import numpy as np
import ml_dtypes


def mxq(x, axis, fmt="e4m3"):
    dtype, down = {"e4m3": (ml_dtypes.float8_e4m3fn, 7), "e5m2": (ml_dtypes.float8_e5m2, 14)}[fmt]
    v = np.moveaxis(np.asarray(x, np.float32).astype(ml_dtypes.bfloat16).astype(np.float64), axis, -1)
    blocks = v.reshape(v.shape[:-1] + (-1, 32))
    amax = np.abs(blocks).max(-1, keepdims=True)
    byte = np.maximum(np.where(amax > 0, np.frexp(amax)[1] - 1 + 127, 0) - down, 1)
    scale = np.exp2(byte - 127.0)
    codes = (blocks / scale).astype(np.float32).astype(dtype).astype(np.float64)
    return np.moveaxis((codes * scale).reshape(v.shape), -1, axis)


WIDE = False


def mx_kscale(k):
    if not WIDE:
        return np.ones(k)
    levels = np.array([10, -10, 5, -5, 0])
    if k % 512:
        return np.exp2(np.random.permutation(np.resize(levels, k // 32))).repeat(32)
    a = np.empty((k // 512, 16))
    for p in range(k // 512):
        a[p, :8] = np.random.permutation(np.resize(levels, 8))
        for g in range(8):
            far = levels[np.abs(levels - a[p, g]) >= 10]
            a[p, g + 8] = far[np.random.randint(len(far))]
    return np.exp2(a.ravel()).repeat(32)


def f64(x):
    return np.asarray(x).astype(np.float64)


def striped(idx):
    return np.tile(idx.reshape(-1, 16).T, (8, 1)).astype(np.uint16)


def unstriped(offs):
    return offs[:16].T.reshape(-1).astype(np.int64)


def striped8(idx):
    return np.concatenate([x.reshape(-1, 16).T for x in idx]).astype(np.uint16)


def runs(offs, k):
    lists = np.stack([offs[16 * r : 16 * r + 16].T.reshape(-1) for r in range(8)]).astype(np.int64)
    return lists[np.arange(k) % 512 // 64]


def pack_weight(w):
    k, n = w.shape
    w = f64(np.asarray(w, np.float32).astype(ml_dtypes.bfloat16)).reshape(k // 32, 32, n)
    amax = np.abs(w).max(1)
    byte = np.clip(np.where(amax > 0, np.frexp(amax)[1] - 1 + 127 - 7, 1), 1, 254)
    scaled = (w * np.exp2(127.0 - byte)[:, None, :]).reshape(k, n).astype(np.float32)
    words = np.ascontiguousarray(scaled.reshape(k // 512, 128, 4, n).transpose(0, 1, 3, 2)).astype(ml_dtypes.float8_e4m3fn).view(np.uint8)
    return words, np.ascontiguousarray(byte.astype(np.uint8).reshape(k // 512, 16, n))


def unpack_weight(words, scales):
    g, p, n, _ = words.shape
    vals = np.ascontiguousarray(words).view(ml_dtypes.float8_e4m3fn).astype(np.float64) * np.repeat(np.exp2(scales.astype(np.float64) - 127.0), 8, axis=1)[..., None]
    return vals.transpose(0, 1, 3, 2).reshape(g * 512, n)

def planes(y):
    n, m = y.shape
    v = y.astype(np.float32).astype(ml_dtypes.bfloat16).astype(np.float64).reshape(n // 32, 32, m)
    top = np.abs(v).max(1)
    byte = np.clip(np.where(top > 0, np.frexp(top)[1] - 1 + 127 - 7, 1), 1, 254)
    codes = (v * np.exp2(127.0 - byte)[:, None, :]).reshape(n, m).astype(np.float32).astype(ml_dtypes.float8_e4m3fn).view(np.uint8)
    words = codes.reshape(n // 512, 128, 4, m).transpose(0, 1, 3, 2)
    return np.ascontiguousarray(words), np.ascontiguousarray(byte.astype(np.uint8).reshape(n // 512, 16, m))


K, T, S, G, H, W, C = 512, 1024, 256, 2048, 512, 128, 512


def setup_inputs():
    n = np.random.standard_normal
    s = mx_kscale(K)[:, None]
    packed_xT = pack_weight(n((K, T)) * s)
    packed_dT = pack_weight(n((K, G)) / s)
    perm = np.random.permutation(S)
    perm2 = np.random.permutation(S)
    return {
        "x_words": packed_xT[0],
        "x_scales": packed_xT[1],
        "d_words": packed_dT[0],
        "d_scales": packed_dT[1],
        "gs": (np.random.uniform(0.5, 1.5, (K, 1)) / s).astype(np.float32),
        "offs": striped8(np.random.randint(0, T, (8, S))),
        "k1": striped8(np.random.randint(0, G, (8, H))),
        "n1": striped(perm[:W]),
        "n2": striped(perm[W:]),
        "n3": striped(np.random.permutation(S)),
        "cand": striped8(np.random.randint(0, T, (8, C))),
        "n4": striped(perm2[:W]),
        "n5": striped(perm2[W:]),
        "n6": striped(np.random.permutation(S)),
    }


def reference(x_words, x_scales, d_words, d_scales, gs, offs, k1, n1, n2, n3, cand, n4, n5, n6):
    x_cand = unpack_weight(x_words, x_scales)[np.arange(K)[:, None], runs(cand, K)]
    d_k1 = unpack_weight(d_words, d_scales)[np.arange(K)[:, None], runs(k1, K)]
    xq = unpack_weight(x_words, x_scales)[np.arange(K)[:, None], runs(offs, K)]
    h = 0.0625 * (d_k1.T @ xq)
    pa = h[:, unstriped(n1)]
    pb = h[:, unstriped(n2)]
    rb = np.minimum(pa, pb)
    ra = np.maximum(pa, pb)
    ds = np.zeros((H, S))
    ds[:, unstriped(n1)] = ra
    dt = ds.copy()
    dt[:, unstriped(n2)] = rb
    z = f64(gs) * (dt - dt[:, unstriped(n3)])
    s = 0.0625 * ((x_cand.T @ mxq(z, 0, "e4m3")))
    pa2 = s[:, unstriped(n4)]
    pb2 = s[:, unstriped(n5)]
    rb2 = pa2 - pb2
    ds2 = np.zeros((C, S))
    ds2[:, unstriped(n4)] = pb2
    dt2 = ds2.copy()
    dt2[:, unstriped(n5)] = rb2
    out_0 = np.maximum(dt2, 0.5 * dt2[:, unstriped(n6)])
    return (out_0,) + planes(out_0)

@@ -1,0 +1,245 @@
+from contextlib import ExitStack
+
+import concourse.mybir as mybir
+
+F32 = mybir.dt.float32
+BF16 = mybir.dt.bfloat16
+I32 = mybir.dt.int32
+U32 = mybir.dt.uint32
+U16 = mybir.dt.uint16
+U8 = mybir.dt.uint8
+FP8X4 = mybir.dt.float8_e4m3fn_x4
+ALU = mybir.AluOpType
+COPY = mybir.ActivationFunctionType.Copy
+
+P = 128
+PACK = 4
+T, G = 1024, 2048
+S = 256
+W = 128
+ROWS = 512
+HALF = S // 2
+PER_COL = 16
+SIXTEENTH = 0.0625
+FLOPS = 2 * 2 * 512 * 512 * 256
+
+
+def tile_picked_hpqhorddswapd_none_po_kernel(
+    tc, x_words, x_scales, d_words, d_scales, gs, offs, k1, n1, n2, n3, cand, n4, n5, n6, out_0, out_1, out_2
+):
+    nc = tc.nc
+    with ExitStack() as ctx:
+        lists = ctx.enter_context(tc.tile_pool(name="lists", bufs=1))
+        sb = ctx.enter_context(tc.tile_pool(name="sb", bufs=1))
+        psum = ctx.enter_context(tc.psum_pool(name="psum", bufs=1))
+
+        def tile(shape, dtype, name, tag=None):
+            return sb.tile(shape, dtype, name=name, tag=tag or name, align_bytes=64)
+
+        def load_list(src, name):
+            held = lists.tile([P, src.shape[1]], U16, name=name)
+            nc.sync.dma_start(held[:], src)
+            return held
+
+        def load_words(src, name):
+            held = tile([P, src.shape[2]], U32, name)
+            nc.sync.dma_start(held[:].bitcast(I32), src[0].rearrange("p n t -> p (n t)").bitcast(I32))
+            return held
+
+        def load_scales(src, name):
+            held = tile([P, src.shape[2]], U8, name)
+            rows = src[0].bitcast(I32)
+            nc.scalar.dma_start(held[:].bitcast(I32), rows.unsqueeze(1).to_broadcast([16, 8, rows.shape[1]]))
+            return held
+
+        def entries(held, start, count):
+            return held[:, start // PER_COL : (start + count) // PER_COL]
+
+        def place_scale_rows(engine, plane):
+            for j in range(1, PACK):
+                engine.dma_start(plane[j:P:32, :].bitcast(I32), plane[8 * j : P : 32, :].bitcast(I32))
+
+        def dealt(ap):
+            return ap.rearrange("p (t m) -> p m t", t=PACK)
+
+        def listed(ap):
+            return ap.rearrange("p (m t) -> p m t", t=PACK)
+
+        d_scale_tab = load_scales(d_scales, "d_scale_tab")
+        x_scale_tab = load_scales(x_scales, "x_scale_tab")
+        k1_l = load_list(k1, "k1_l")
+        offs_l = load_list(offs, "offs_l")
+        d_word_tab = load_words(d_words, "d_word_tab")
+        x_word_tab = load_words(x_words, "x_word_tab")
+        n1_l = load_list(n1, "n1_l")
+        n2_l = load_list(n2, "n2_l")
+        cand_l = load_list(cand, "cand_l")
+        n3_l = load_list(n3, "n3_l")
+        n4_l = load_list(n4, "n4_l")
+        n5_l = load_list(n5, "n5_l")
+        n6_l = load_list(n6, "n6_l")
+        gs_sb = tile([P, PACK], F32, "gs_sb")
+        nc.sync.dma_start(gs_sb[:], gs.rearrange("(p t) o -> p (t o)", t=PACK))
+
+        d_bytes = tile([P, ROWS], U8, "d_bytes")
+        xq_bytes = tile([P, S], U8, "xq_bytes")
+        plane1 = tile([P, ROWS + S], U8, "plane1")
+        nc.vector.tensor_copy(d_bytes[:], d_scale_tab[:].indirect(k1_l[:]))
+        nc.vector.tensor_copy(xq_bytes[:], x_scale_tab[:].indirect(offs_l[:]))
+        nc.vector.tensor_copy(dealt(plane1[:, 0:ROWS]), listed(d_bytes[:]))
+        nc.vector.tensor_copy(plane1[:, ROWS : ROWS + S].bitcast(I32), xq_bytes[:].bitcast(I32))
+        place_scale_rows(nc.scalar, plane1)
+
+        d_picked = tile([P, ROWS], U32, "d_picked")
+        xq_picked = tile([P, S], U32, "xq_picked")
+        d_first = tile([P, P], U32, "d_first")
+        d_rest = tile([P, PACK - 1, P], U32, "d_rest")
+        nc.vector.tensor_copy(d_picked[:], d_word_tab[:].indirect(k1_l[:]))
+        nc.vector.tensor_copy(xq_picked[:], x_word_tab[:].indirect(offs_l[:]))
+        d_view = listed(d_picked[:].bitcast(I32))
+        nc.vector.tensor_copy(d_first[:].bitcast(I32), d_view[:, :, 0])
+        nc.vector.tensor_copy(d_rest[:].bitcast(I32).rearrange("p t m -> p m t"), d_view[:, :, 1:PACK])
+
+        h = []
+        for t in range(PACK):
+            bank = psum.tile([P, S], F32, name=f"h_bank{t}")
+            words = d_first[:] if t == 0 else d_rest[:, t - 1, :]
+            nc.tensor.matmul_mx(
+                out=bank[:],
+                lhsT=words.bitcast(FP8X4),
+                lhsT_scale=plane1[:, t * P : (t + 1) * P],
+                rhs=xq_picked[:].bitcast(FP8X4),
+                rhs_scale=plane1[:, ROWS : ROWS + S],
+                start=True,
+                stop=True,
+            )
+            h_t = tile([P, S], F32, f"h{t}")
+            if t == 0:
+                nc.scalar.activation(h_t[:], bank[:], COPY, scale=SIXTEENTH)
+            else:
+                nc.vector.tensor_scalar(h_t[:], bank[:], SIXTEENTH, None, ALU.mult)
+            h.append(h_t)
+
+        def pair_stage(src, first_l, second_l, combine, name):
+            pa = [tile([P, W], F32, f"{name}_pa{t}") for t in range(PACK)]
+            pb = [tile([P, W], F32, f"{name}_pb{t}") for t in range(PACK)]
+            dst = [tile([P, S], F32, f"{name}_dt{t}") for t in range(PACK)]
+            made = []
+
+            def fetch_a(t):
+                nc.scalar.activation(pa[t][:], src[t][:].indirect(first_l[:]), COPY)
+
+            def fetch_b(t):
+                nc.scalar.activation(pb[t][:], src[t][:].indirect(second_l[:]), COPY)
+                made.append(combine(t, pa[t], pb[t]))
+
+            def put_a(t):
+                nc.scalar.activation(dst[t][:].indirect(first_l[:]), made[t][0][:], COPY)
+
+            def put_b(t):
+                nc.scalar.activation(dst[t][:].indirect(second_l[:]), made[t][1][:], COPY)
+
+            for t in (0, 1):
+                fetch_a(t)
+                fetch_b(t)
+            for t in (0, 1):
+                put_a(t)
+                fetch_a(t + 2)
+                put_b(t)
+                fetch_b(t + 2)
+            for put in (put_a, put_b):
+                for t in (2, 3):
+                    put(t)
+            return dst
+
+        def sort_pair(t, pa, pb):
+            ra = tile([P, W], F32, f"ra{t}")
+            rb = tile([P, W], F32, f"rb{t}")
+            nc.vector.tensor_tensor(ra[:], pa[:], pb[:], ALU.max)
+            nc.vector.tensor_tensor(rb[:], pa[:], pb[:], ALU.min)
+            return ra, rb
+
+        dt = pair_stage(h, n1_l, n2_l, sort_pair, "one")
+
+        c_picked = tile([P, ROWS], U32, "c_picked", tag="h0")
+        c_bytes = tile([P, ROWS], U8, "c_bytes", tag="h1")
+        c_words = tile([P, ROWS], U32, "c_words")
+        plane2 = tile([P, ROWS], U8, "plane2")
+        for lo in range(0, ROWS, S):
+            nc.vector.tensor_copy(c_bytes[:, lo : lo + S], x_scale_tab[:].indirect(entries(cand_l, lo, S)))
+        nc.vector.tensor_copy(dealt(plane2[:]), listed(c_bytes[:]))
+        place_scale_rows(nc.sync, plane2)
+        for lo in range(0, ROWS, S):
+            nc.vector.tensor_copy(c_picked[:, lo : lo + S], x_word_tab[:].indirect(entries(cand_l, lo, S)))
+        nc.vector.tensor_copy(dealt(c_words[:].bitcast(I32)), listed(c_picked[:].bitcast(I32)))
+
+        weighted = tile([P, PACK, S], F32, "weighted")
+        for t in range(PACK):
+            nc.vector.tensor_scalar(weighted[:, t, :], dt[t][:], gs_sb[:, t : t + 1], None, ALU.mult)
+        other = tile([P, 2, PACK, HALF], F32, "other", tag="rb3")
+        s = [tile([P, S], F32, f"s{t}") for t in range(PACK)]
+        for half in range(2):
+            cols = slice(half * HALF, (half + 1) * HALF)
+            for t in range(PACK):
+                nc.scalar.activation(other[:, half, t, :], weighted[:, t, :].indirect(entries(n3_l, half * HALF, HALF)), COPY)
+            z_bf = tile([P, HALF, PACK], BF16, f"z_bf{half}")
+            z_words = tile([P, HALF], U32, f"z_words{half}")
+            z_scales = tile([P, HALF], U8, f"z_scales{half}")
+            nc.vector.tensor_tensor(
+                z_bf[:].rearrange("p (c i) t -> p c t i", i=4),
+                weighted[:, :, cols].rearrange("p t (c i) -> p c t i", i=4),
+                other[:, half, :, :].rearrange("p t (c i) -> p c t i", i=4),
+                ALU.subtract,
+            )
+            nc.vector.quantize_mx(out=z_words[:].bitcast(FP8X4), scales=z_scales[:], in_=z_bf[:].rearrange("p c t -> p (c t)"))
+            banks = []
+            for t in range(PACK):
+                bank = psum.tile([P, HALF], F32, name=f"s_bank{half}{t}", tag=f"h_bank{t}" if half == 0 else f"s_bank{t}")
+                nc.tensor.matmul_mx(
+                    out=bank[:],
+                    lhsT=c_words[:, t * P : (t + 1) * P].bitcast(FP8X4),
+                    lhsT_scale=plane2[:, t * P : (t + 1) * P],
+                    rhs=z_words[:].bitcast(FP8X4),
+                    rhs_scale=z_scales[:],
+                    start=True,
+                    stop=True,
+                )
+                banks.append(bank)
+            if half == 0:
+                first_banks = banks
+        for t in range(PACK):
+            nc.scalar.activation(s[t][:, 0:HALF], first_banks[t][:], COPY, scale=SIXTEENTH)
+        nc.scalar.activation(s[0][:, HALF:S], banks[0][:], COPY, scale=SIXTEENTH)
+        for t in range(1, PACK):
+            nc.vector.tensor_scalar(s[t][:, HALF:S], banks[t][:], SIXTEENTH, None, ALU.mult)
+
+        def swap_diff(t, pa, pb):
+            rb = tile([P, W], F32, f"rb2_{t}")
+            nc.vector.tensor_tensor(rb[:], pa[:], pb[:], ALU.subtract)
+            return pb, rb
+
+        dt2 = pair_stage(s, n4_l, n5_l, swap_diff, "two")
+
+        other2 = tile([P, 2, PACK, HALF], F32, "other2", tag="rb2_3")
+        y = tile([P, PACK, S], F32, "y")
+        y_words = tile([P, S], U32, "y_words")
+        y_scales = tile([P, S], U8, "y_scales")
+        out_rows = out_0.rearrange("(p t) c -> p t c", t=PACK)
+        out_words = out_1[0].rearrange("p n t -> p (n t)").bitcast(I32)
+        for half in range(2):
+            cols = slice(half * HALF, (half + 1) * HALF)
+            for t in range(PACK):
+                nc.scalar.activation(other2[:, half, t, :], dt2[t][:].indirect(entries(n6_l, half * HALF, HALF)), COPY)
+                nc.vector.scalar_tensor_tensor(y[:, t, cols], other2[:, half, t, :], 0.5, dt2[t][:, cols], ALU.mult, ALU.max)
+                if half == 1:
+                    nc.sync.dma_start(out_rows[:, t, :], y[:, t, :])
+            y_bf = tile([P, HALF, PACK], BF16, f"y_bf{half}")
+            nc.vector.tensor_copy(
+                y_bf[:].rearrange("p (c i) t -> p c t i", i=4),
+                y[:, :, cols].rearrange("p t (c i) -> p c t i", i=4),
+            )
+            nc.vector.quantize_mx(out=y_words[:, cols].bitcast(FP8X4), scales=y_scales[:, cols], in_=y_bf[:].rearrange("p c t -> p (c t)"))
+        nc.scalar.dma_start(out_words, y_words[:].bitcast(I32))
+        for q in range(4):
+            engine = nc.sync if q < 2 else nc.scalar
+            engine.dma_start(out_2[0, 4 * q : 4 * q + 4, :].bitcast(I32), y_scales[32 * q : 32 * q + 4, :].bitcast(I32))

@@ -19,6 +19,7 @@ S = 256
 W = 128
 ROWS = 512
 HALF = S // 2
+LAST = 192
 PER_COL = 16
 SIXTEENTH = 0.0625
 FLOPS = 2 * 2 * 512 * 512 * 256
@@ -55,8 +56,8 @@ def tile_picked_hpqhorddswapd_none_po_kernel(
         def entries(held, start, count):
             return held[:, start // PER_COL : (start + count) // PER_COL]
 
-        def place_scale_rows(engine, plane):
-            for j in range(1, PACK):
+        def place_scale_rows(engines, plane):
+            for j, engine in zip(range(1, PACK), engines):
                 engine.dma_start(plane[j:P:32, :].bitcast(I32), plane[8 * j : P : 32, :].bitcast(I32))
 
         def dealt(ap):
@@ -65,162 +66,151 @@ def tile_picked_hpqhorddswapd_none_po_kernel(
         def listed(ap):
             return ap.rearrange("p (m t) -> p m t", t=PACK)
 
-        d_scale_tab = load_scales(d_scales, "d_scale_tab")
         x_scale_tab = load_scales(x_scales, "x_scale_tab")
-        k1_l = load_list(k1, "k1_l")
+        d_scale_tab = load_scales(d_scales, "d_scale_tab")
         offs_l = load_list(offs, "offs_l")
-        d_word_tab = load_words(d_words, "d_word_tab")
-        x_word_tab = load_words(x_words, "x_word_tab")
+        k1_l = load_list(k1, "k1_l")
         n1_l = load_list(n1, "n1_l")
         n2_l = load_list(n2, "n2_l")
         cand_l = load_list(cand, "cand_l")
+        d_word_tab = load_words(d_words, "d_word_tab")
+        x_word_tab = load_words(x_words, "x_word_tab")
         n3_l = load_list(n3, "n3_l")
         n4_l = load_list(n4, "n4_l")
         n5_l = load_list(n5, "n5_l")
         n6_l = load_list(n6, "n6_l")
-        gs_sb = tile([P, PACK], F32, "gs_sb")
-        nc.sync.dma_start(gs_sb[:], gs.rearrange("(p t) o -> p (t o)", t=PACK))
 
         d_bytes = tile([P, ROWS], U8, "d_bytes")
         xq_bytes = tile([P, S], U8, "xq_bytes")
         plane1 = tile([P, ROWS + S], U8, "plane1")
-        nc.vector.tensor_copy(d_bytes[:], d_scale_tab[:].indirect(k1_l[:]))
         nc.vector.tensor_copy(xq_bytes[:], x_scale_tab[:].indirect(offs_l[:]))
-        nc.vector.tensor_copy(dealt(plane1[:, 0:ROWS]), listed(d_bytes[:]))
         nc.vector.tensor_copy(plane1[:, ROWS : ROWS + S].bitcast(I32), xq_bytes[:].bitcast(I32))
-        place_scale_rows(nc.scalar, plane1)
+        nc.vector.tensor_copy(d_bytes[:], d_scale_tab[:].indirect(k1_l[:]))
+        nc.vector.tensor_copy(dealt(plane1[:, 0:ROWS]), listed(d_bytes[:]))
+        place_scale_rows((nc.sync, nc.scalar, nc.sync), plane1)
 
         d_picked = tile([P, ROWS], U32, "d_picked")
         xq_picked = tile([P, S], U32, "xq_picked")
-        d_first = tile([P, P], U32, "d_first")
-        d_rest = tile([P, PACK - 1, P], U32, "d_rest")
         nc.vector.tensor_copy(d_picked[:], d_word_tab[:].indirect(k1_l[:]))
-        nc.vector.tensor_copy(xq_picked[:], x_word_tab[:].indirect(offs_l[:]))
+        for lo in range(0, S, HALF):
+            nc.vector.tensor_copy(xq_picked[:, lo : lo + HALF], x_word_tab[:].indirect(entries(offs_l, lo, HALF)))
         d_view = listed(d_picked[:].bitcast(I32))
-        nc.vector.tensor_copy(d_first[:].bitcast(I32), d_view[:, :, 0])
-        nc.vector.tensor_copy(d_rest[:].bitcast(I32).rearrange("p t m -> p m t"), d_view[:, :, 1:PACK])
 
-        h = []
-        for t in range(PACK):
-            bank = psum.tile([P, S], F32, name=f"h_bank{t}")
-            words = d_first[:] if t == 0 else d_rest[:, t - 1, :]
+        def h_product(bank, words, t, cols):
             nc.tensor.matmul_mx(
                 out=bank[:],
                 lhsT=words.bitcast(FP8X4),
                 lhsT_scale=plane1[:, t * P : (t + 1) * P],
-                rhs=xq_picked[:].bitcast(FP8X4),
-                rhs_scale=plane1[:, ROWS : ROWS + S],
+                rhs=xq_picked[:, cols].bitcast(FP8X4),
+                rhs_scale=plane1[:, ROWS + cols.start : ROWS + cols.stop],
                 start=True,
                 stop=True,
             )
-            h_t = tile([P, S], F32, f"h{t}")
-            if t == 0:
-                nc.scalar.activation(h_t[:], bank[:], COPY, scale=SIXTEENTH)
-            else:
-                nc.vector.tensor_scalar(h_t[:], bank[:], SIXTEENTH, None, ALU.mult)
-            h.append(h_t)
 
-        def pair_stage(src, first_l, second_l, combine, name):
+        h = [tile([P, S], F32, f"h{t}") for t in range(PACK)]
+        for t in range(PACK):
+            if t % 2 == 0:
+                d_two = tile([P, 2, P], U32, f"d_two{t}", tag="d_two")
+                nc.vector.tensor_copy(d_two[:].bitcast(I32).rearrange("p t m -> p m t"), d_view[:, :, t : t + 2])
+            if t == 0:
+                for lo in range(0, S, HALF):
+                    cols = slice(lo, lo + HALF)
+                    bank = psum.tile([P, HALF], F32, name=f"h_first{lo}", tag=f"bank{4 * lo // HALF}")
+                    h_product(bank, d_two[:, 0, :], 0, cols)
+                    nc.scalar.activation(h[0][:, cols], bank[:], COPY, scale=SIXTEENTH)
+            else:
+                bank = psum.tile([P, S], F32, name=f"h_bank{t}", tag=f"bank{t}")
+                h_product(bank, d_two[:, t % 2, :], t, slice(0, S))
+                nc.vector.tensor_scalar(h[t][:], bank[:], SIXTEENTH, None, ALU.mult)
+
+        def fetch_pairs(src, first_l, second_l, name):
             pa = [tile([P, W], F32, f"{name}_pa{t}") for t in range(PACK)]
             pb = [tile([P, W], F32, f"{name}_pb{t}") for t in range(PACK)]
-            dst = [tile([P, S], F32, f"{name}_dt{t}") for t in range(PACK)]
-            made = []
-
-            def fetch_a(t):
+            for t in range(PACK):
                 nc.scalar.activation(pa[t][:], src[t][:].indirect(first_l[:]), COPY)
-
-            def fetch_b(t):
                 nc.scalar.activation(pb[t][:], src[t][:].indirect(second_l[:]), COPY)
-                made.append(combine(t, pa[t], pb[t]))
+            return pa, pb
 
-            def put_a(t):
-                nc.scalar.activation(dst[t][:].indirect(first_l[:]), made[t][0][:], COPY)
-
-            def put_b(t):
-                nc.scalar.activation(dst[t][:].indirect(second_l[:]), made[t][1][:], COPY)
-
-            for t in (0, 1):
-                fetch_a(t)
-                fetch_b(t)
-            for t in (0, 1):
-                put_a(t)
-                fetch_a(t + 2)
-                put_b(t)
-                fetch_b(t + 2)
-            for put in (put_a, put_b):
-                for t in (2, 3):
-                    put(t)
+        def put_pairs(first, first_l, second, second_l, name):
+            dst = [tile([P, S], F32, f"{name}{t}") for t in range(PACK)]
+            for two in ((0, 1), (2, 3)):
+                for values, places in ((first, first_l), (second, second_l)):
+                    for t in two:
+                        nc.scalar.activation(dst[t][:].indirect(places[:]), values[t][:], COPY)
             return dst
 
-        def sort_pair(t, pa, pb):
-            ra = tile([P, W], F32, f"ra{t}")
-            rb = tile([P, W], F32, f"rb{t}")
-            nc.vector.tensor_tensor(ra[:], pa[:], pb[:], ALU.max)
-            nc.vector.tensor_tensor(rb[:], pa[:], pb[:], ALU.min)
-            return ra, rb
+        pa, pb = fetch_pairs(h, n1_l, n2_l, "one")
+        ra = [tile([P, W], F32, f"ra{t}") for t in range(PACK)]
+        rb = [tile([P, W], F32, f"rb{t}") for t in range(PACK)]
+        for two in ((0, 1), (2, 3)):
+            for result, op in ((ra, ALU.max), (rb, ALU.min)):
+                for t in two:
+                    nc.vector.tensor_tensor(result[t][:], pa[t][:], pb[t][:], op)
+        dt = put_pairs(ra, n1_l, rb, n2_l, "dt")
 
-        dt = pair_stage(h, n1_l, n2_l, sort_pair, "one")
-
-        c_picked = tile([P, ROWS], U32, "c_picked", tag="h0")
-        c_bytes = tile([P, ROWS], U8, "c_bytes", tag="h1")
+        c_picked = tile([P, ROWS], U32, "c_picked", tag="one_pb3")
+        c_bytes = tile([P, ROWS], U8, "c_bytes", tag="one_pa3")
         c_words = tile([P, ROWS], U32, "c_words")
         plane2 = tile([P, ROWS], U8, "plane2")
         for lo in range(0, ROWS, S):
             nc.vector.tensor_copy(c_bytes[:, lo : lo + S], x_scale_tab[:].indirect(entries(cand_l, lo, S)))
         nc.vector.tensor_copy(dealt(plane2[:]), listed(c_bytes[:]))
-        place_scale_rows(nc.sync, plane2)
+        place_scale_rows((nc.sync, nc.sync, nc.sync), plane2)
         for lo in range(0, ROWS, S):
             nc.vector.tensor_copy(c_picked[:, lo : lo + S], x_word_tab[:].indirect(entries(cand_l, lo, S)))
         nc.vector.tensor_copy(dealt(c_words[:].bitcast(I32)), listed(c_picked[:].bitcast(I32)))
 
+        gs_sb = tile([P, PACK], F32, "gs_sb", tag="xq_picked")
+        nc.sync.dma_start(gs_sb[:], gs.rearrange("(p t) o -> p (t o)", t=PACK))
         weighted = tile([P, PACK, S], F32, "weighted")
         for t in range(PACK):
             nc.vector.tensor_scalar(weighted[:, t, :], dt[t][:], gs_sb[:, t : t + 1], None, ALU.mult)
-        other = tile([P, 2, PACK, HALF], F32, "other", tag="rb3")
         s = [tile([P, S], F32, f"s{t}") for t in range(PACK)]
+        z_words = tile([P, S], U32, "z_words")
+        z_scales = tile([P, S], U8, "z_scales")
+        other_head = tile([P, PACK * HALF], F32, "other_head", tag="rb2")
+        other_tail = tile([P, PACK * HALF], F32, "other_tail", tag="dt3")
+        for lo, hi in ((0, HALF), (HALF, LAST), (LAST, S)):
+            width = hi - lo
+            room = other_head[:] if lo == 0 else other_tail[:, PACK * (lo - HALF) : PACK * (hi - HALF)]
+            other = room.rearrange("p (t c) -> p t c", t=PACK)
+            for t in range(PACK):
+                nc.scalar.activation(other[:, t, :], weighted[:, t, :].indirect(entries(n3_l, lo, width)), COPY)
+            z_bf = tile([P, width, PACK], BF16, f"z_bf{lo}")
+            nc.vector.tensor_tensor(
+                z_bf[:].rearrange("p (c i) t -> p c t i", i=4),
+                weighted[:, :, lo:hi].rearrange("p t (c i) -> p c t i", i=4),
+                other.rearrange("p t (c i) -> p c t i", i=4),
+                ALU.subtract,
+            )
+            nc.vector.quantize_mx(
+                out=z_words[:, lo:hi].bitcast(FP8X4), scales=z_scales[:, lo:hi], in_=z_bf[:].rearrange("p c t -> p (c t)")
+            )
         for half in range(2):
             cols = slice(half * HALF, (half + 1) * HALF)
             for t in range(PACK):
-                nc.scalar.activation(other[:, half, t, :], weighted[:, t, :].indirect(entries(n3_l, half * HALF, HALF)), COPY)
-            z_bf = tile([P, HALF, PACK], BF16, f"z_bf{half}")
-            z_words = tile([P, HALF], U32, f"z_words{half}")
-            z_scales = tile([P, HALF], U8, f"z_scales{half}")
-            nc.vector.tensor_tensor(
-                z_bf[:].rearrange("p (c i) t -> p c t i", i=4),
-                weighted[:, :, cols].rearrange("p t (c i) -> p c t i", i=4),
-                other[:, half, :, :].rearrange("p t (c i) -> p c t i", i=4),
-                ALU.subtract,
-            )
-            nc.vector.quantize_mx(out=z_words[:].bitcast(FP8X4), scales=z_scales[:], in_=z_bf[:].rearrange("p c t -> p (c t)"))
-            banks = []
-            for t in range(PACK):
-                bank = psum.tile([P, HALF], F32, name=f"s_bank{half}{t}", tag=f"h_bank{t}" if half == 0 else f"s_bank{t}")
+                bank = psum.tile([P, HALF], F32, name=f"s_bank{half}{t}", tag=f"bank{PACK * half + t}")
                 nc.tensor.matmul_mx(
                     out=bank[:],
                     lhsT=c_words[:, t * P : (t + 1) * P].bitcast(FP8X4),
                     lhsT_scale=plane2[:, t * P : (t + 1) * P],
-                    rhs=z_words[:].bitcast(FP8X4),
-                    rhs_scale=z_scales[:],
+                    rhs=z_words[:, cols].bitcast(FP8X4),
+                    rhs_scale=z_scales[:, cols],
                     start=True,
                     stop=True,
                 )
-                banks.append(bank)
-            if half == 0:
-                first_banks = banks
+                if half == 0 or t == 0:
+                    nc.scalar.activation(s[t][:, cols], bank[:], COPY, scale=SIXTEENTH)
+                else:
+                    nc.vector.tensor_scalar(s[t][:, cols], bank[:], SIXTEENTH, None, ALU.mult)
+
+        pa2, pb2 = fetch_pairs(s, n4_l, n5_l, "two")
+        rb2 = [tile([P, W], F32, f"rb2_{t}") for t in range(PACK)]
         for t in range(PACK):
-            nc.scalar.activation(s[t][:, 0:HALF], first_banks[t][:], COPY, scale=SIXTEENTH)
-        nc.scalar.activation(s[0][:, HALF:S], banks[0][:], COPY, scale=SIXTEENTH)
-        for t in range(1, PACK):
-            nc.vector.tensor_scalar(s[t][:, HALF:S], banks[t][:], SIXTEENTH, None, ALU.mult)
+            nc.vector.tensor_tensor(rb2[t][:], pa2[t][:], pb2[t][:], ALU.subtract)
+        dt2 = put_pairs(pb2, n4_l, rb2, n5_l, "dt2_")
 
-        def swap_diff(t, pa, pb):
-            rb = tile([P, W], F32, f"rb2_{t}")
-            nc.vector.tensor_tensor(rb[:], pa[:], pb[:], ALU.subtract)
-            return pb, rb
-
-        dt2 = pair_stage(s, n4_l, n5_l, swap_diff, "two")
-
-        other2 = tile([P, 2, PACK, HALF], F32, "other2", tag="rb2_3")
+        other2 = tile([P, 2, PACK, HALF], F32, "other2", tag="rb2_2")
         y = tile([P, PACK, S], F32, "y")
         y_words = tile([P, S], U32, "y_words")
         y_scales = tile([P, S], U8, "y_scales")
@@ -231,15 +221,18 @@ def tile_picked_hpqhorddswapd_none_po_kernel(
             for t in range(PACK):
                 nc.scalar.activation(other2[:, half, t, :], dt2[t][:].indirect(entries(n6_l, half * HALF, HALF)), COPY)
                 nc.vector.scalar_tensor_tensor(y[:, t, cols], other2[:, half, t, :], 0.5, dt2[t][:, cols], ALU.mult, ALU.max)
-                if half == 1:
-                    nc.sync.dma_start(out_rows[:, t, :], y[:, t, :])
-            y_bf = tile([P, HALF, PACK], BF16, f"y_bf{half}")
+                if half == 1 and t >= 2:
+                    rows = slice(0, 3) if t == 2 else slice(3, 4)
+                    nc.sync.dma_start(out_rows[:, rows, cols], y[:, rows, cols])
+            if half == 0:
+                nc.sync.dma_start(out_rows[:, :, cols], y[:, :, cols])
+            y_bf = tile([P, HALF, PACK], BF16, f"y_bf{half}", tag="y_bf")
             nc.vector.tensor_copy(
                 y_bf[:].rearrange("p (c i) t -> p c t i", i=4),
                 y[:, :, cols].rearrange("p t (c i) -> p c t i", i=4),
             )
             nc.vector.quantize_mx(out=y_words[:, cols].bitcast(FP8X4), scales=y_scales[:, cols], in_=y_bf[:].rearrange("p c t -> p (c t)"))
-        nc.scalar.dma_start(out_words, y_words[:].bitcast(I32))
+            nc.sync.dma_start(out_words[:, cols], y_words[:, cols].bitcast(I32))
         for q in range(4):
-            engine = nc.sync if q < 2 else nc.scalar
+            engine = nc.sync if q < 1 else nc.scalar
             engine.dma_start(out_2[0, 4 * q : 4 * q + 4, :].bitcast(I32), y_scales[32 * q : 32 * q + 4, :].bitcast(I32))

@@ -44,7 +44,7 @@ def tile_picked_hpqhorddswapd_none_po_kernel(
 
         def load_words(src, name):
             held = tile([P, src.shape[2]], U32, name)
-            nc.sync.dma_start(held[:].bitcast(I32), src[0].rearrange("p n t -> p (n t)").bitcast(I32))
+            nc.scalar.dma_start(held[:].bitcast(I32), src[0].rearrange("p n t -> p (n t)").bitcast(I32))
             return held
 
         def load_scales(src, name):
@@ -74,6 +74,8 @@ def tile_picked_hpqhorddswapd_none_po_kernel(
         n2_l = load_list(n2, "n2_l")
         cand_l = load_list(cand, "cand_l")
         d_word_tab = load_words(d_words, "d_word_tab")
+        gs_sb = tile([P, PACK], F32, "gs_sb")
+        nc.scalar.dma_start(gs_sb[:], gs.rearrange("(p t) o -> p (t o)", t=PACK))
         x_word_tab = load_words(x_words, "x_word_tab")
         n3_l = load_list(n3, "n3_l")
         n4_l = load_list(n4, "n4_l")
@@ -85,8 +87,10 @@ def tile_picked_hpqhorddswapd_none_po_kernel(
         plane1 = tile([P, ROWS + S], U8, "plane1")
         nc.vector.tensor_copy(xq_bytes[:], x_scale_tab[:].indirect(offs_l[:]))
         nc.vector.tensor_copy(plane1[:, ROWS : ROWS + S].bitcast(I32), xq_bytes[:].bitcast(I32))
-        nc.vector.tensor_copy(d_bytes[:], d_scale_tab[:].indirect(k1_l[:]))
-        nc.vector.tensor_copy(dealt(plane1[:, 0:ROWS]), listed(d_bytes[:]))
+        for lo in range(0, ROWS, S):
+            nc.vector.tensor_copy(d_bytes[:, lo : lo + S], d_scale_tab[:].indirect(entries(k1_l, lo, S)))
+        for lo in range(0, ROWS, S):
+            nc.vector.tensor_copy(dealt(plane1[:, 0:ROWS])[:, lo // PACK : (lo + S) // PACK, :], listed(d_bytes[:, lo : lo + S]))
         place_scale_rows((nc.sync, nc.scalar, nc.sync), plane1)
 
         d_picked = tile([P, ROWS], U32, "d_picked")
@@ -160,8 +164,6 @@ def tile_picked_hpqhorddswapd_none_po_kernel(
             nc.vector.tensor_copy(c_picked[:, lo : lo + S], x_word_tab[:].indirect(entries(cand_l, lo, S)))
         nc.vector.tensor_copy(dealt(c_words[:].bitcast(I32)), listed(c_picked[:].bitcast(I32)))
 
-        gs_sb = tile([P, PACK], F32, "gs_sb", tag="xq_picked")
-        nc.sync.dma_start(gs_sb[:], gs.rearrange("(p t) o -> p (t o)", t=PACK))
         weighted = tile([P, PACK, S], F32, "weighted")
         for t in range(PACK):
             nc.vector.tensor_scalar(weighted[:, t, :], dt[t][:], gs_sb[:, t : t + 1], None, ALU.mult)
@@ -210,29 +212,45 @@ def tile_picked_hpqhorddswapd_none_po_kernel(
             nc.vector.tensor_tensor(rb2[t][:], pa2[t][:], pb2[t][:], ALU.subtract)
         dt2 = put_pairs(pb2, n4_l, rb2, n5_l, "dt2_")
 
-        other2 = tile([P, 2, PACK, HALF], F32, "other2", tag="rb2_2")
+        other2 = tile([P, PACK, S], F32, "other2", tag="rb2_2")
         y = tile([P, PACK, S], F32, "y")
         y_words = tile([P, S], U32, "y_words")
         y_scales = tile([P, S], U8, "y_scales")
         out_rows = out_0.rearrange("(p t) c -> p t c", t=PACK)
         out_words = out_1[0].rearrange("p n t -> p (n t)").bitcast(I32)
-        for half in range(2):
-            cols = slice(half * HALF, (half + 1) * HALF)
-            for t in range(PACK):
-                nc.scalar.activation(other2[:, half, t, :], dt2[t][:].indirect(entries(n6_l, half * HALF, HALF)), COPY)
-                nc.vector.scalar_tensor_tensor(y[:, t, cols], other2[:, half, t, :], 0.5, dt2[t][:, cols], ALU.mult, ALU.max)
-                if half == 1 and t >= 2:
-                    rows = slice(0, 3) if t == 2 else slice(3, 4)
-                    nc.sync.dma_start(out_rows[:, rows, cols], y[:, rows, cols])
-            if half == 0:
-                nc.sync.dma_start(out_rows[:, :, cols], y[:, :, cols])
-            y_bf = tile([P, HALF, PACK], BF16, f"y_bf{half}", tag="y_bf")
+        def fetch_and_max(t, lo, hi):
+            nc.scalar.activation(other2[:, t, lo:hi], dt2[t][:].indirect(entries(n6_l, lo, hi - lo)), COPY)
+            nc.vector.scalar_tensor_tensor(y[:, t, lo:hi], other2[:, t, lo:hi], 0.5, dt2[t][:, lo:hi], ALU.mult, ALU.max)
+
+        def round_y(lo, hi):
+            y_bf = tile([P, hi - lo, PACK], BF16, f"y_bf{lo}")
             nc.vector.tensor_copy(
                 y_bf[:].rearrange("p (c i) t -> p c t i", i=4),
-                y[:, :, cols].rearrange("p t (c i) -> p c t i", i=4),
+                y[:, :, lo:hi].rearrange("p t (c i) -> p c t i", i=4),
             )
-            nc.vector.quantize_mx(out=y_words[:, cols].bitcast(FP8X4), scales=y_scales[:, cols], in_=y_bf[:].rearrange("p c t -> p (c t)"))
-            nc.sync.dma_start(out_words[:, cols], y_words[:, cols].bitcast(I32))
+            return y_bf
+
+        def quantise_y(y_bf, lo, hi):
+            nc.vector.quantize_mx(
+                out=y_words[:, lo:hi].bitcast(FP8X4), scales=y_scales[:, lo:hi], in_=y_bf[:].rearrange("p c t -> p (c t)")
+            )
+
+        for t in range(PACK):
+            fetch_and_max(t, 0, HALF)
+        nc.sync.dma_start(out_rows[:, :, 0:HALF], y[:, :, 0:HALF])
+        quantise_y(round_y(0, HALF), 0, HALF)
+        nc.sync.dma_start(out_words[:, 0:HALF], y_words[:, 0:HALF].bitcast(I32))
+        for t in range(PACK - 1):
+            fetch_and_max(t, HALF, S)
+        nc.sync.dma_start(out_rows[:, 0 : PACK - 1, HALF:S], y[:, 0 : PACK - 1, HALF:S])
+        pieces = ((HALF, LAST), (LAST, S))
+        for lo, hi in pieces:
+            fetch_and_max(PACK - 1, lo, hi)
+        nc.sync.dma_start(out_rows[:, PACK - 1, HALF:S], y[:, PACK - 1, HALF:S])
+        rounded = [round_y(lo, hi) for lo, hi in pieces]
+        for y_bf, (lo, hi) in zip(rounded, pieces):
+            quantise_y(y_bf, lo, hi)
+        nc.sync.dma_start(out_words[:, HALF:S], y_words[:, HALF:S].bitcast(I32))
         for q in range(4):
-            engine = nc.sync if q < 1 else nc.scalar
+            engine = nc.scalar if q < 2 else nc.sync
             engine.dma_start(out_2[0, 4 * q : 4 * q + 4, :].bitcast(I32), y_scales[32 * q : 32 * q + 4, :].bitcast(I32))

from contextlib import ExitStack

import concourse.mybir as mybir

F32 = mybir.dt.float32
BF16 = mybir.dt.bfloat16
I32 = mybir.dt.int32
U32 = mybir.dt.uint32
U16 = mybir.dt.uint16
U8 = mybir.dt.uint8
FP8X4 = mybir.dt.float8_e4m3fn_x4
ALU = mybir.AluOpType
COPY = mybir.ActivationFunctionType.Copy

P = 128
PACK = 4
T, G = 1024, 2048
S = 256
W = 128
ROWS = 512
HALF = S // 2
LAST = 192
PER_COL = 16
SIXTEENTH = 0.0625
FLOPS = 2 * 2 * 512 * 512 * 256


def tile_picked_hpqhorddswapd_none_po_kernel(
    tc, x_words, x_scales, d_words, d_scales, gs, offs, k1, n1, n2, n3, cand, n4, n5, n6, out_0, out_1, out_2
):
    nc = tc.nc
    with ExitStack() as ctx:
        lists = ctx.enter_context(tc.tile_pool(name="lists", bufs=1))
        sb = ctx.enter_context(tc.tile_pool(name="sb", bufs=1))
        psum = ctx.enter_context(tc.psum_pool(name="psum", bufs=1))

        def tile(shape, dtype, name, tag=None):
            return sb.tile(shape, dtype, name=name, tag=tag or name, align_bytes=64)

        def load_list(src, name):
            held = lists.tile([P, src.shape[1]], U16, name=name)
            nc.sync.dma_start(held[:], src)
            return held

        def load_words(src, name):
            held = tile([P, src.shape[2]], U32, name)
            nc.scalar.dma_start(held[:].bitcast(I32), src[0].rearrange("p n t -> p (n t)").bitcast(I32))
            return held

        def load_scales(src, name):
            held = tile([P, src.shape[2]], U8, name)
            rows = src[0].bitcast(I32)
            nc.scalar.dma_start(held[:].bitcast(I32), rows.unsqueeze(1).to_broadcast([16, 8, rows.shape[1]]))
            return held

        def entries(held, start, count):
            return held[:, start // PER_COL : (start + count) // PER_COL]

        def place_scale_rows(engines, plane):
            for j, engine in zip(range(1, PACK), engines):
                engine.dma_start(plane[j:P:32, :].bitcast(I32), plane[8 * j : P : 32, :].bitcast(I32))

        def dealt(ap):
            return ap.rearrange("p (t m) -> p m t", t=PACK)

        def listed(ap):
            return ap.rearrange("p (m t) -> p m t", t=PACK)

        x_scale_tab = load_scales(x_scales, "x_scale_tab")
        d_scale_tab = load_scales(d_scales, "d_scale_tab")
        offs_l = load_list(offs, "offs_l")
        k1_l = load_list(k1, "k1_l")
        n1_l = load_list(n1, "n1_l")
        n2_l = load_list(n2, "n2_l")
        cand_l = load_list(cand, "cand_l")
        d_word_tab = load_words(d_words, "d_word_tab")
        gs_sb = tile([P, PACK], F32, "gs_sb")
        nc.scalar.dma_start(gs_sb[:], gs.rearrange("(p t) o -> p (t o)", t=PACK))
        x_word_tab = load_words(x_words, "x_word_tab")
        n3_l = load_list(n3, "n3_l")
        n4_l = load_list(n4, "n4_l")
        n5_l = load_list(n5, "n5_l")
        n6_l = load_list(n6, "n6_l")

        d_bytes = tile([P, ROWS], U8, "d_bytes")
        xq_bytes = tile([P, S], U8, "xq_bytes")
        plane1 = tile([P, ROWS + S], U8, "plane1")
        nc.vector.tensor_copy(xq_bytes[:], x_scale_tab[:].indirect(offs_l[:]))
        nc.vector.tensor_copy(plane1[:, ROWS : ROWS + S].bitcast(I32), xq_bytes[:].bitcast(I32))
        for lo in range(0, ROWS, S):
            nc.vector.tensor_copy(d_bytes[:, lo : lo + S], d_scale_tab[:].indirect(entries(k1_l, lo, S)))
        for lo in range(0, ROWS, S):
            nc.vector.tensor_copy(dealt(plane1[:, 0:ROWS])[:, lo // PACK : (lo + S) // PACK, :], listed(d_bytes[:, lo : lo + S]))
        place_scale_rows((nc.sync, nc.scalar, nc.sync), plane1)

        d_picked = tile([P, ROWS], U32, "d_picked")
        xq_picked = tile([P, S], U32, "xq_picked")
        nc.vector.tensor_copy(d_picked[:], d_word_tab[:].indirect(k1_l[:]))
        for lo in range(0, S, HALF):
            nc.vector.tensor_copy(xq_picked[:, lo : lo + HALF], x_word_tab[:].indirect(entries(offs_l, lo, HALF)))
        d_view = listed(d_picked[:].bitcast(I32))

        def h_product(bank, words, t, cols):
            nc.tensor.matmul_mx(
                out=bank[:],
                lhsT=words.bitcast(FP8X4),
                lhsT_scale=plane1[:, t * P : (t + 1) * P],
                rhs=xq_picked[:, cols].bitcast(FP8X4),
                rhs_scale=plane1[:, ROWS + cols.start : ROWS + cols.stop],
                start=True,
                stop=True,
            )

        h = [tile([P, S], F32, f"h{t}") for t in range(PACK)]
        for t in range(PACK):
            if t % 2 == 0:
                d_two = tile([P, 2, P], U32, f"d_two{t}", tag="d_two")
                nc.vector.tensor_copy(d_two[:].bitcast(I32).rearrange("p t m -> p m t"), d_view[:, :, t : t + 2])
            if t == 0:
                for lo in range(0, S, HALF):
                    cols = slice(lo, lo + HALF)
                    bank = psum.tile([P, HALF], F32, name=f"h_first{lo}", tag=f"bank{4 * lo // HALF}")
                    h_product(bank, d_two[:, 0, :], 0, cols)
                    nc.scalar.activation(h[0][:, cols], bank[:], COPY, scale=SIXTEENTH)
            else:
                bank = psum.tile([P, S], F32, name=f"h_bank{t}", tag=f"bank{t}")
                h_product(bank, d_two[:, t % 2, :], t, slice(0, S))
                nc.vector.tensor_scalar(h[t][:], bank[:], SIXTEENTH, None, ALU.mult)

        def fetch_pairs(src, first_l, second_l, name):
            pa = [tile([P, W], F32, f"{name}_pa{t}") for t in range(PACK)]
            pb = [tile([P, W], F32, f"{name}_pb{t}") for t in range(PACK)]
            for t in range(PACK):
                nc.scalar.activation(pa[t][:], src[t][:].indirect(first_l[:]), COPY)
                nc.scalar.activation(pb[t][:], src[t][:].indirect(second_l[:]), COPY)
            return pa, pb

        def put_pairs(first, first_l, second, second_l, name):
            dst = [tile([P, S], F32, f"{name}{t}") for t in range(PACK)]
            for two in ((0, 1), (2, 3)):
                for values, places in ((first, first_l), (second, second_l)):
                    for t in two:
                        nc.scalar.activation(dst[t][:].indirect(places[:]), values[t][:], COPY)
            return dst

        pa, pb = fetch_pairs(h, n1_l, n2_l, "one")
        ra = [tile([P, W], F32, f"ra{t}") for t in range(PACK)]
        rb = [tile([P, W], F32, f"rb{t}") for t in range(PACK)]
        for two in ((0, 1), (2, 3)):
            for result, op in ((ra, ALU.max), (rb, ALU.min)):
                for t in two:
                    nc.vector.tensor_tensor(result[t][:], pa[t][:], pb[t][:], op)
        dt = put_pairs(ra, n1_l, rb, n2_l, "dt")

        c_picked = tile([P, ROWS], U32, "c_picked", tag="one_pb3")
        c_bytes = tile([P, ROWS], U8, "c_bytes", tag="one_pa3")
        c_words = tile([P, ROWS], U32, "c_words")
        plane2 = tile([P, ROWS], U8, "plane2")
        for lo in range(0, ROWS, S):
            nc.vector.tensor_copy(c_bytes[:, lo : lo + S], x_scale_tab[:].indirect(entries(cand_l, lo, S)))
        nc.vector.tensor_copy(dealt(plane2[:]), listed(c_bytes[:]))
        place_scale_rows((nc.sync, nc.sync, nc.sync), plane2)
        for lo in range(0, ROWS, S):
            nc.vector.tensor_copy(c_picked[:, lo : lo + S], x_word_tab[:].indirect(entries(cand_l, lo, S)))
        nc.vector.tensor_copy(dealt(c_words[:].bitcast(I32)), listed(c_picked[:].bitcast(I32)))

        weighted = tile([P, PACK, S], F32, "weighted")
        for t in range(PACK):
            nc.vector.tensor_scalar(weighted[:, t, :], dt[t][:], gs_sb[:, t : t + 1], None, ALU.mult)
        s = [tile([P, S], F32, f"s{t}") for t in range(PACK)]
        z_words = tile([P, S], U32, "z_words")
        z_scales = tile([P, S], U8, "z_scales")
        other_head = tile([P, PACK * HALF], F32, "other_head", tag="rb2")
        other_tail = tile([P, PACK * HALF], F32, "other_tail", tag="dt3")
        for lo, hi in ((0, HALF), (HALF, LAST), (LAST, S)):
            width = hi - lo
            room = other_head[:] if lo == 0 else other_tail[:, PACK * (lo - HALF) : PACK * (hi - HALF)]
            other = room.rearrange("p (t c) -> p t c", t=PACK)
            for t in range(PACK):
                nc.scalar.activation(other[:, t, :], weighted[:, t, :].indirect(entries(n3_l, lo, width)), COPY)
            z_bf = tile([P, width, PACK], BF16, f"z_bf{lo}")
            nc.vector.tensor_tensor(
                z_bf[:].rearrange("p (c i) t -> p c t i", i=4),
                weighted[:, :, lo:hi].rearrange("p t (c i) -> p c t i", i=4),
                other.rearrange("p t (c i) -> p c t i", i=4),
                ALU.subtract,
            )
            nc.vector.quantize_mx(
                out=z_words[:, lo:hi].bitcast(FP8X4), scales=z_scales[:, lo:hi], in_=z_bf[:].rearrange("p c t -> p (c t)")
            )
        for half in range(2):
            cols = slice(half * HALF, (half + 1) * HALF)
            for t in range(PACK):
                bank = psum.tile([P, HALF], F32, name=f"s_bank{half}{t}", tag=f"bank{PACK * half + t}")
                nc.tensor.matmul_mx(
                    out=bank[:],
                    lhsT=c_words[:, t * P : (t + 1) * P].bitcast(FP8X4),
                    lhsT_scale=plane2[:, t * P : (t + 1) * P],
                    rhs=z_words[:, cols].bitcast(FP8X4),
                    rhs_scale=z_scales[:, cols],
                    start=True,
                    stop=True,
                )
                if half == 0 or t == 0:
                    nc.scalar.activation(s[t][:, cols], bank[:], COPY, scale=SIXTEENTH)
                else:
                    nc.vector.tensor_scalar(s[t][:, cols], bank[:], SIXTEENTH, None, ALU.mult)

        pa2, pb2 = fetch_pairs(s, n4_l, n5_l, "two")
        rb2 = [tile([P, W], F32, f"rb2_{t}") for t in range(PACK)]
        for t in range(PACK):
            nc.vector.tensor_tensor(rb2[t][:], pa2[t][:], pb2[t][:], ALU.subtract)
        dt2 = put_pairs(pb2, n4_l, rb2, n5_l, "dt2_")

        other2 = tile([P, PACK, S], F32, "other2", tag="rb2_2")
        y = tile([P, PACK, S], F32, "y")
        y_words = tile([P, S], U32, "y_words")
        y_scales = tile([P, S], U8, "y_scales")
        out_rows = out_0.rearrange("(p t) c -> p t c", t=PACK)
        out_words = out_1[0].rearrange("p n t -> p (n t)").bitcast(I32)
        def fetch_and_max(t, lo, hi):
            nc.scalar.activation(other2[:, t, lo:hi], dt2[t][:].indirect(entries(n6_l, lo, hi - lo)), COPY)
            nc.vector.scalar_tensor_tensor(y[:, t, lo:hi], other2[:, t, lo:hi], 0.5, dt2[t][:, lo:hi], ALU.mult, ALU.max)

        def round_y(lo, hi):
            y_bf = tile([P, hi - lo, PACK], BF16, f"y_bf{lo}")
            nc.vector.tensor_copy(
                y_bf[:].rearrange("p (c i) t -> p c t i", i=4),
                y[:, :, lo:hi].rearrange("p t (c i) -> p c t i", i=4),
            )
            return y_bf

        def quantise_y(y_bf, lo, hi):
            nc.vector.quantize_mx(
                out=y_words[:, lo:hi].bitcast(FP8X4), scales=y_scales[:, lo:hi], in_=y_bf[:].rearrange("p c t -> p (c t)")
            )

        for t in range(PACK):
            fetch_and_max(t, 0, HALF)
        nc.sync.dma_start(out_rows[:, :, 0:HALF], y[:, :, 0:HALF])
        quantise_y(round_y(0, HALF), 0, HALF)
        nc.sync.dma_start(out_words[:, 0:HALF], y_words[:, 0:HALF].bitcast(I32))
        for t in range(PACK - 1):
            fetch_and_max(t, HALF, S)
        nc.sync.dma_start(out_rows[:, 0 : PACK - 1, HALF:S], y[:, 0 : PACK - 1, HALF:S])
        pieces = ((HALF, LAST), (LAST, S))
        for lo, hi in pieces:
            fetch_and_max(PACK - 1, lo, hi)
        nc.sync.dma_start(out_rows[:, PACK - 1, HALF:S], y[:, PACK - 1, HALF:S])
        rounded = [round_y(lo, hi) for lo, hi in pieces]
        for y_bf, (lo, hi) in zip(rounded, pieces):
            quantise_y(y_bf, lo, hi)
        nc.sync.dma_start(out_words[:, HALF:S], y_words[:, HALF:S].bitcast(I32))
        for q in range(4):
            engine = nc.scalar if q < 2 else nc.sync
            engine.dma_start(out_2[0, 4 * q : 4 * q + 4, :].bitcast(I32), y_scales[32 * q : 32 * q + 4, :].bitcast(I32))
